import numpy as np
import ml_dtypes

BF16 = ml_dtypes.bfloat16


def bf(x):
    return np.asarray(x, np.float32).astype(BF16)


def f32(x):
    return np.asarray(x, np.float32)


def f64(x):
    return np.asarray(x).astype(np.float64)


def striped(idx):
    return np.tile(idx.reshape(-1, 16).T, (8, 1))


S, K, M, N, E, Q = 512, 256, 128, 384, 4, 96


def setup_inputs():
    return {"base": bf(np.random.standard_normal((M, S))), "x": bf(np.random.standard_normal((K, N))), "w": bf(np.random.standard_normal((E, K, M)) / np.sqrt(K)), "b": f32(0.5 * np.random.standard_normal((M, 1))), "offs": striped(np.random.permutation(S)[:N])}


def reference(base, x, w, b, offs):
    idx = offs[:16].T.reshape(-1)
    z = f64(base).copy()
    for e in range(E):
        z[:, idx[e * Q : (e + 1) * Q]] += f64(w)[e].T @ f64(x)[:, e * Q : (e + 1) * Q]
    return np.tanh(z + f64(b))

@@ -1,0 +1,59 @@
+import concourse.mybir as mybir
+from concourse.masks import make_identity
+
+BF16, F32, U16 = mybir.dt.bfloat16, mybir.dt.float32, mybir.dt.uint16
+TANH = mybir.ActivationFunctionType.Tanh
+
+P = 128
+S = 512
+K = 256
+KB = K // P
+N = 384
+E = 4
+Q = N // E
+QC = Q // 16
+
+FLOPS = 2 * K * P * N
+
+
+def tile_scatter_matmul_kernel(tc, base, x, w, b, offs, out):
+    nc = tc.nc
+    with (
+        tc.tile_pool(name="held", bufs=1) as held,
+        tc.psum_pool(name="psum", bufs=1) as psum,
+    ):
+        offsets = held.tile([P, N // 16], U16, name="offsets")
+        nc.sync.dma_start(offsets[:], offs)
+
+        base_sb = held.tile([P, S], BF16, name="base_sb")
+        nc.sync.dma_start(base_sb[:], base)
+
+        x_sb = held.tile([P, KB, N], BF16, name="x_sb")
+        nc.scalar.dma_start(x_sb[:], x.rearrange("(kb p) n -> p kb n", p=P))
+
+        bias = held.tile([P, 1], F32, name="bias")
+        nc.scalar.dma_start(bias[:], b)
+
+        w_sb = held.tile([P, E * KB, P], BF16, name="w_sb")
+        nc.gpsimd.dma_start(w_sb[:], w.rearrange("e (kb p) m -> p (e kb) m", p=P))
+
+        ident = held.tile([P, P], BF16, name="ident")
+        make_identity(nc, ident[:])
+
+        window = psum.tile([P, S], F32, name="window")
+        nc.tensor.matmul(window[:], ident[:], base_sb[:], start=True, stop=False)
+
+        for e in range(E):
+            piece = offsets[:, e * QC : (e + 1) * QC]
+            for kb in range(KB):
+                nc.tensor.matmul(
+                    window[:].indirect(piece),
+                    w_sb[:, e * KB + kb, :],
+                    x_sb[:, kb, e * Q : (e + 1) * Q],
+                    start=False,
+                    stop=(e == E - 1 and kb == KB - 1),
+                )
+
+        result = held.tile([P, S], F32, name="result")
+        nc.scalar.activation(result[:], window[:], TANH, bias=bias[:, 0:1])
+        nc.sync.dma_start(out, result[:])

@@ -13,6 +13,11 @@ E = 4
 Q = N // E
 QC = Q // 16
 
+WARM_COLUMNS = 256
+WARM_MATMULS = 6
+
+HALF = S // 2
+
 FLOPS = 2 * K * P * N
 
 
@@ -23,22 +28,30 @@ def tile_scatter_matmul_kernel(tc, base, x, w, b, offs, out):
         tc.psum_pool(name="psum", bufs=1) as psum,
     ):
         offsets = held.tile([P, N // 16], U16, name="offsets")
-        nc.sync.dma_start(offsets[:], offs)
-
         base_sb = held.tile([P, S], BF16, name="base_sb")
-        nc.sync.dma_start(base_sb[:], base)
-
         x_sb = held.tile([P, KB, N], BF16, name="x_sb")
-        nc.scalar.dma_start(x_sb[:], x.rearrange("(kb p) n -> p kb n", p=P))
-
+        w_sb = [held.tile([P, KB, P], BF16, name="w_sb%d" % e) for e in range(E)]
         bias = held.tile([P, 1], F32, name="bias")
-        nc.scalar.dma_start(bias[:], b)
 
-        w_sb = held.tile([P, E * KB, P], BF16, name="w_sb")
-        nc.gpsimd.dma_start(w_sb[:], w.rearrange("e (kb p) m -> p (e kb) m", p=P))
+        nc.sync.dma_start(offsets[:], offs)
+        nc.scalar.dma_start(base_sb[:], base)
+        nc.sync.dma_start(x_sb[:], x.rearrange("(p kb) n -> p kb n", p=P))
+        for e in range(E):
+            queue = nc.scalar if e % 2 == 0 else nc.sync
+            queue.dma_start(w_sb[e][:], w[e].rearrange("(p kb) m -> p kb m", p=P))
 
         ident = held.tile([P, P], BF16, name="ident")
         make_identity(nc, ident[:])
+        nc.gpsimd.dma_start(bias[:], b)
+
+        zeros = held.tile([P, WARM_COLUMNS], BF16, name="zeros")
+        nc.vector.memset(zeros[:], 0.0)
+        warm = held.tile([P, 1], F32, name="warm")
+        nc.scalar.activation(warm[:], zeros[:, 0:1], TANH)
+
+        idle_bank = psum.tile([P, WARM_COLUMNS], F32, name="idle_bank")
+        for i in range(WARM_MATMULS):
+            nc.tensor.matmul(idle_bank[:], zeros[:, 0:P], zeros[:], start=True, stop=True)
 
         window = psum.tile([P, S], F32, name="window")
         nc.tensor.matmul(window[:], ident[:], base_sb[:], start=True, stop=False)
@@ -48,12 +61,14 @@ def tile_scatter_matmul_kernel(tc, base, x, w, b, offs, out):
             for kb in range(KB):
                 nc.tensor.matmul(
                     window[:].indirect(piece),
-                    w_sb[:, e * KB + kb, :],
+                    w_sb[e][:, kb, :],
                     x_sb[:, kb, e * Q : (e + 1) * Q],
                     start=False,
                     stop=(e == E - 1 and kb == KB - 1),
                 )
 
-        result = held.tile([P, S], F32, name="result")
-        nc.scalar.activation(result[:], window[:], TANH, bias=bias[:, 0:1])
-        nc.sync.dma_start(out, result[:])
+        for h, queue in enumerate((nc.sync, nc.scalar)):
+            columns = slice(h * HALF, (h + 1) * HALF)
+            result = held.tile([P, HALF], F32, name="result%d" % h)
+            nc.scalar.activation(result[:], window[:, columns], TANH, bias=bias[:, 0:1])
+            queue.dma_start(out[:, columns], result[:])

@@ -33,12 +33,11 @@ def tile_scatter_matmul_kernel(tc, base, x, w, b, offs, out):
         w_sb = [held.tile([P, KB, P], BF16, name="w_sb%d" % e) for e in range(E)]
         bias = held.tile([P, 1], F32, name="bias")
 
+        nc.sync.dma_start(base_sb[:], base)
         nc.sync.dma_start(offsets[:], offs)
-        nc.scalar.dma_start(base_sb[:], base)
         nc.sync.dma_start(x_sb[:], x.rearrange("(p kb) n -> p kb n", p=P))
         for e in range(E):
-            queue = nc.scalar if e % 2 == 0 else nc.sync
-            queue.dma_start(w_sb[e][:], w[e].rearrange("(p kb) m -> p kb m", p=P))
+            nc.sync.dma_start(w_sb[e][:], w[e].rearrange("(p kb) m -> p kb m", p=P))
 
         ident = held.tile([P, P], BF16, name="ident")
         make_identity(nc, ident[:])

@@ -14,7 +14,7 @@ Q = N // E
 QC = Q // 16
 
 WARM_COLUMNS = 256
-WARM_MATMULS = 6
+WARM_MATMULS = 7
 
 HALF = S // 2
 
@@ -43,14 +43,16 @@ def tile_scatter_matmul_kernel(tc, base, x, w, b, offs, out):
         make_identity(nc, ident[:])
         nc.gpsimd.dma_start(bias[:], b)
 
-        zeros = held.tile([P, WARM_COLUMNS], BF16, name="zeros")
+        zeros = held.tile([P, 2], BF16, name="zeros")
         nc.vector.memset(zeros[:], 0.0)
         warm = held.tile([P, 1], F32, name="warm")
         nc.scalar.activation(warm[:], zeros[:, 0:1], TANH)
 
         idle_bank = psum.tile([P, WARM_COLUMNS], F32, name="idle_bank")
+        zero_weights = zeros[:, 0:1].to_broadcast([P, P])
+        zero_columns = zeros[:, 0:1].to_broadcast([P, WARM_COLUMNS])
         for i in range(WARM_MATMULS):
-            nc.tensor.matmul(idle_bank[:], zeros[:, 0:P], zeros[:], start=True, stop=True)
+            nc.tensor.matmul(idle_bank[:], zero_weights, zero_columns, start=True, stop=True)
 
         window = psum.tile([P, S], F32, name="window")
         nc.tensor.matmul(window[:], ident[:], base_sb[:], start=True, stop=False)

@@ -18,6 +18,8 @@ WARM_MATMULS = 7
 
 HALF = S // 2
 
+BLOCK = 32
+
 FLOPS = 2 * K * P * N
 
 
@@ -31,7 +33,6 @@ def tile_scatter_matmul_kernel(tc, base, x, w, b, offs, out):
         base_sb = held.tile([P, S], BF16, name="base_sb")
         x_sb = held.tile([P, KB, N], BF16, name="x_sb")
         w_sb = [held.tile([P, KB, P], BF16, name="w_sb%d" % e) for e in range(E)]
-        bias = held.tile([P, 1], F32, name="bias")
 
         nc.sync.dma_start(base_sb[:], base)
         nc.sync.dma_start(offsets[:], offs)
@@ -41,12 +42,18 @@ def tile_scatter_matmul_kernel(tc, base, x, w, b, offs, out):
 
         ident = held.tile([P, P], BF16, name="ident")
         make_identity(nc, ident[:])
-        nc.gpsimd.dma_start(bias[:], b)
 
         zeros = held.tile([P, 2], BF16, name="zeros")
         nc.vector.memset(zeros[:], 0.0)
         warm = held.tile([P, 1], F32, name="warm")
         nc.scalar.activation(warm[:], zeros[:, 0:1], TANH)
+
+        b_rows = held.tile([P, BLOCK], F32, name="b_rows", align_bytes=64)
+        nc.vector.memset(b_rows[:], 0.0)
+        nc.scalar.dma_start(b_rows[0:P:BLOCK, :], b.rearrange("(q i) o -> q (i o)", i=BLOCK))
+        b_cols = held.tile([P, BLOCK], F32, name="b_cols", align_bytes=64)
+        nc.vector.transpose(b_cols[:], b_rows[:])
+        bias = b_cols[:, 0:1]
 
         idle_bank = psum.tile([P, WARM_COLUMNS], F32, name="idle_bank")
         zero_weights = zeros[:, 0:1].to_broadcast([P, P])
@@ -71,5 +78,5 @@ def tile_scatter_matmul_kernel(tc, base, x, w, b, offs, out):
         for h, queue in enumerate((nc.sync, nc.scalar)):
             columns = slice(h * HALF, (h + 1) * HALF)
             result = held.tile([P, HALF], F32, name="result%d" % h)
-            nc.scalar.activation(result[:], window[:, columns], TANH, bias=bias[:, 0:1])
+            nc.scalar.activation(result[:], window[:, columns], TANH, bias=bias)
             queue.dma_start(out[:, columns], result[:])

@@ -1,8 +1,8 @@
 import concourse.mybir as mybir
-from concourse.masks import make_identity
 
 BF16, F32, U16 = mybir.dt.bfloat16, mybir.dt.float32, mybir.dt.uint16
 TANH = mybir.ActivationFunctionType.Tanh
+MULT, ADD, IS_EQUAL = mybir.AluOpType.mult, mybir.AluOpType.add, mybir.AluOpType.is_equal
 
 P = 128
 S = 512
@@ -40,9 +40,6 @@ def tile_scatter_matmul_kernel(tc, base, x, w, b, offs, out):
         for e in range(E):
             nc.sync.dma_start(w_sb[e][:], w[e].rearrange("(p kb) m -> p kb m", p=P))
 
-        ident = held.tile([P, P], BF16, name="ident")
-        make_identity(nc, ident[:])
-
         zeros = held.tile([P, 2], BF16, name="zeros")
         nc.vector.memset(zeros[:], 0.0)
         warm = held.tile([P, 1], F32, name="warm")
@@ -54,6 +51,20 @@ def tile_scatter_matmul_kernel(tc, base, x, w, b, offs, out):
         b_cols = held.tile([P, BLOCK], F32, name="b_cols", align_bytes=64)
         nc.vector.transpose(b_cols[:], b_rows[:])
         bias = b_cols[:, 0:1]
+
+        ones = held.tile([P, BLOCK], F32, name="ones")
+        nc.vector.memset(ones[:], 1.0)
+        count = held.tile([P, BLOCK], F32, name="count", align_bytes=64)
+        nc.vector.tensor_tensor_scan(count[:], ones[:], ones[:], 0.0, MULT, ADD)
+        own = held.tile([P, BLOCK], F32, name="own", align_bytes=64)
+        nc.vector.transpose(own[:], count[:])
+        ident = held.tile([P, P], BF16, name="ident")
+        nc.vector.memset(ident[:], 0.0)
+        for q in range(P // BLOCK):
+            block = slice(q * BLOCK, (q + 1) * BLOCK)
+            nc.vector.tensor_scalar(
+                ident[block, block], count[block, :], own[block, 0:1], None, IS_EQUAL
+            )
 
         idle_bank = psum.tile([P, WARM_COLUMNS], F32, name="idle_bank")
         zero_weights = zeros[:, 0:1].to_broadcast([P, P])

@@ -45,26 +45,26 @@ def tile_scatter_matmul_kernel(tc, base, x, w, b, offs, out):
         warm = held.tile([P, 1], F32, name="warm")
         nc.scalar.activation(warm[:], zeros[:, 0:1], TANH)
 
-        b_rows = held.tile([P, BLOCK], F32, name="b_rows", align_bytes=64)
-        nc.vector.memset(b_rows[:], 0.0)
-        nc.scalar.dma_start(b_rows[0:P:BLOCK, :], b.rearrange("(q i) o -> q (i o)", i=BLOCK))
-        b_cols = held.tile([P, BLOCK], F32, name="b_cols", align_bytes=64)
-        nc.vector.transpose(b_cols[:], b_rows[:])
-        bias = b_cols[:, 0:1]
-
         ones = held.tile([P, BLOCK], F32, name="ones")
-        nc.vector.memset(ones[:], 1.0)
         count = held.tile([P, BLOCK], F32, name="count", align_bytes=64)
-        nc.vector.tensor_tensor_scan(count[:], ones[:], ones[:], 0.0, MULT, ADD)
         own = held.tile([P, BLOCK], F32, name="own", align_bytes=64)
-        nc.vector.transpose(own[:], count[:])
         ident = held.tile([P, P], BF16, name="ident")
+        b_rows = held.tile([P, BLOCK], F32, name="b_rows", align_bytes=64)
+        nc.vector.memset(ones[:], 1.0)
+        nc.vector.tensor_tensor_scan(count[:], ones[:], ones[:], 0.0, MULT, ADD)
         nc.vector.memset(ident[:], 0.0)
+        nc.vector.transpose(own[:], count[:])
+        nc.vector.memset(b_rows[:], 0.0)
         for q in range(P // BLOCK):
             block = slice(q * BLOCK, (q + 1) * BLOCK)
             nc.vector.tensor_scalar(
                 ident[block, block], count[block, :], own[block, 0:1], None, IS_EQUAL
             )
+
+        nc.scalar.dma_start(b_rows[0:P:BLOCK, :], b.rearrange("(q i) o -> q (i o)", i=BLOCK))
+        b_cols = held.tile([P, BLOCK], F32, name="b_cols", align_bytes=64)
+        nc.vector.transpose(b_cols[:], b_rows[:])
+        bias = b_cols[:, 0:1]
 
         idle_bank = psum.tile([P, WARM_COLUMNS], F32, name="idle_bank")
         zero_weights = zeros[:, 0:1].to_broadcast([P, P])

@@ -61,7 +61,7 @@ def tile_scatter_matmul_kernel(tc, base, x, w, b, offs, out):
                 ident[block, block], count[block, :], own[block, 0:1], None, IS_EQUAL
             )
 
-        nc.scalar.dma_start(b_rows[0:P:BLOCK, :], b.rearrange("(q i) o -> q (i o)", i=BLOCK))
+        nc.sync.dma_start(b_rows[0:P:BLOCK, :], b.rearrange("(q i) o -> q (i o)", i=BLOCK))
         b_cols = held.tile([P, BLOCK], F32, name="b_cols", align_bytes=64)
         nc.vector.transpose(b_cols[:], b_rows[:])
         bias = b_cols[:, 0:1]

@@ -10,6 +10,7 @@ K = 256
 KB = K // P
 N = 384
 E = 4
+PAIR = 2
 Q = N // E
 QC = Q // 16
 
@@ -32,13 +33,14 @@ def tile_scatter_matmul_kernel(tc, base, x, w, b, offs, out):
         offsets = held.tile([P, N // 16], U16, name="offsets")
         base_sb = held.tile([P, S], BF16, name="base_sb")
         x_sb = held.tile([P, KB, N], BF16, name="x_sb")
-        w_sb = [held.tile([P, KB, P], BF16, name="w_sb%d" % e) for e in range(E)]
+        w_sb = [held.tile([P, PAIR, KB, P], BF16, name="w_sb%d" % g) for g in range(E // PAIR)]
 
         nc.sync.dma_start(base_sb[:], base)
         nc.sync.dma_start(offsets[:], offs)
         nc.sync.dma_start(x_sb[:], x.rearrange("(p kb) n -> p kb n", p=P))
-        for e in range(E):
-            nc.sync.dma_start(w_sb[e][:], w[e].rearrange("(p kb) m -> p kb m", p=P))
+        for g in range(E // PAIR):
+            pair = w[g * PAIR : (g + 1) * PAIR]
+            nc.sync.dma_start(w_sb[g][:], pair.rearrange("e (p kb) m -> p e kb m", p=P))
 
         zeros = held.tile([P, 2], BF16, name="zeros")
         nc.vector.memset(zeros[:], 0.0)
@@ -80,7 +82,7 @@ def tile_scatter_matmul_kernel(tc, base, x, w, b, offs, out):
             for kb in range(KB):
                 nc.tensor.matmul(
                     window[:].indirect(piece),
-                    w_sb[e][:, kb, :],
+                    w_sb[e // PAIR][:, e % PAIR, kb, :],
                     x_sb[:, kb, e * Q : (e + 1) * Q],
                     start=False,
                     stop=(e == E - 1 and kb == KB - 1),

@@ -88,8 +88,8 @@ def tile_scatter_matmul_kernel(tc, base, x, w, b, offs, out):
                     stop=(e == E - 1 and kb == KB - 1),
                 )
 
-        for h, queue in enumerate((nc.sync, nc.scalar)):
+        for h in range(S // HALF):
             columns = slice(h * HALF, (h + 1) * HALF)
             result = held.tile([P, HALF], F32, name="result%d" % h)
             nc.scalar.activation(result[:], window[:, columns], TANH, bias=bias)
-            queue.dma_start(out[:, columns], result[:])
+            nc.scalar.dma_start(out[:, columns], result[:])

@@ -21,6 +21,8 @@ HALF = S // 2
 
 BLOCK = 32
 
+BURST = 256
+
 FLOPS = 2 * K * P * N
 
 
@@ -31,9 +33,12 @@ def tile_scatter_matmul_kernel(tc, base, x, w, b, offs, out):
         tc.psum_pool(name="psum", bufs=1) as psum,
     ):
         offsets = held.tile([P, N // 16], U16, name="offsets")
-        base_sb = held.tile([P, S], BF16, name="base_sb")
-        x_sb = held.tile([P, KB, N], BF16, name="x_sb")
-        w_sb = [held.tile([P, PAIR, KB, P], BF16, name="w_sb%d" % g) for g in range(E // PAIR)]
+        base_sb = held.tile([P, S], BF16, name="base_sb", align_bytes=BURST)
+        x_sb = held.tile([P, KB, N], BF16, name="x_sb", align_bytes=BURST)
+        w_sb = [
+            held.tile([P, PAIR, KB, P], BF16, name="w_sb%d" % g, align_bytes=BURST)
+            for g in range(E // PAIR)
+        ]
 
         nc.sync.dma_start(base_sb[:], base)
         nc.sync.dma_start(offsets[:], offs)
@@ -90,6 +95,6 @@ def tile_scatter_matmul_kernel(tc, base, x, w, b, offs, out):
 
         for h in range(S // HALF):
             columns = slice(h * HALF, (h + 1) * HALF)
-            result = held.tile([P, HALF], F32, name="result%d" % h)
+            result = held.tile([P, HALF], F32, name="result%d" % h, align_bytes=BURST)
             nc.scalar.activation(result[:], window[:, columns], TANH, bias=bias)
             nc.scalar.dma_start(out[:, columns], result[:])

@@ -21,7 +21,7 @@ HALF = S // 2
 
 BLOCK = 32
 
-BURST = 256
+KIB = 1024
 
 FLOPS = 2 * K * P * N
 
@@ -33,10 +33,10 @@ def tile_scatter_matmul_kernel(tc, base, x, w, b, offs, out):
         tc.psum_pool(name="psum", bufs=1) as psum,
     ):
         offsets = held.tile([P, N // 16], U16, name="offsets")
-        base_sb = held.tile([P, S], BF16, name="base_sb", align_bytes=BURST)
-        x_sb = held.tile([P, KB, N], BF16, name="x_sb", align_bytes=BURST)
+        base_sb = held.tile([P, S], BF16, name="base_sb", align_bytes=KIB)
+        x_sb = held.tile([P, KB, N], BF16, name="x_sb", align_bytes=2 * KIB)
         w_sb = [
-            held.tile([P, PAIR, KB, P], BF16, name="w_sb%d" % g, align_bytes=BURST)
+            held.tile([P, PAIR, KB, P], BF16, name="w_sb%d" % g, align_bytes=KIB)
             for g in range(E // PAIR)
         ]
 
@@ -95,6 +95,6 @@ def tile_scatter_matmul_kernel(tc, base, x, w, b, offs, out):
 
         for h in range(S // HALF):
             columns = slice(h * HALF, (h + 1) * HALF)
-            result = held.tile([P, HALF], F32, name="result%d" % h, align_bytes=BURST)
+            result = held.tile([P, HALF], F32, name="result%d" % h, align_bytes=KIB)
             nc.scalar.activation(result[:], window[:, columns], TANH, bias=bias)
             nc.scalar.dma_start(out[:, columns], result[:])

import concourse.mybir as mybir

BF16, F32, U16 = mybir.dt.bfloat16, mybir.dt.float32, mybir.dt.uint16
TANH = mybir.ActivationFunctionType.Tanh
MULT, ADD, IS_EQUAL = mybir.AluOpType.mult, mybir.AluOpType.add, mybir.AluOpType.is_equal

P = 128
S = 512
K = 256
KB = K // P
N = 384
E = 4
PAIR = 2
Q = N // E
QC = Q // 16

WARM_COLUMNS = 256
WARM_MATMULS = 7

HALF = S // 2

BLOCK = 32

KIB = 1024

FLOPS = 2 * K * P * N


def tile_scatter_matmul_kernel(tc, base, x, w, b, offs, out):
    nc = tc.nc
    with (
        tc.tile_pool(name="held", bufs=1) as held,
        tc.psum_pool(name="psum", bufs=1) as psum,
    ):
        offsets = held.tile([P, N // 16], U16, name="offsets")
        base_sb = held.tile([P, S], BF16, name="base_sb", align_bytes=KIB)
        x_sb = held.tile([P, KB, N], BF16, name="x_sb", align_bytes=2 * KIB)
        w_sb = [
            held.tile([P, PAIR, KB, P], BF16, name="w_sb%d" % g, align_bytes=KIB)
            for g in range(E // PAIR)
        ]

        nc.sync.dma_start(base_sb[:], base)
        nc.sync.dma_start(offsets[:], offs)
        nc.sync.dma_start(x_sb[:], x.rearrange("(p kb) n -> p kb n", p=P))
        for g in range(E // PAIR):
            pair = w[g * PAIR : (g + 1) * PAIR]
            nc.sync.dma_start(w_sb[g][:], pair.rearrange("e (p kb) m -> p e kb m", p=P))

        zeros = held.tile([P, 2], BF16, name="zeros")
        nc.vector.memset(zeros[:], 0.0)
        warm = held.tile([P, 1], F32, name="warm")
        nc.scalar.activation(warm[:], zeros[:, 0:1], TANH)

        ones = held.tile([P, BLOCK], F32, name="ones")
        count = held.tile([P, BLOCK], F32, name="count", align_bytes=64)
        own = held.tile([P, BLOCK], F32, name="own", align_bytes=64)
        ident = held.tile([P, P], BF16, name="ident")
        b_rows = held.tile([P, BLOCK], F32, name="b_rows", align_bytes=64)
        nc.vector.memset(ones[:], 1.0)
        nc.vector.tensor_tensor_scan(count[:], ones[:], ones[:], 0.0, MULT, ADD)
        nc.vector.memset(ident[:], 0.0)
        nc.vector.transpose(own[:], count[:])
        nc.vector.memset(b_rows[:], 0.0)
        for q in range(P // BLOCK):
            block = slice(q * BLOCK, (q + 1) * BLOCK)
            nc.vector.tensor_scalar(
                ident[block, block], count[block, :], own[block, 0:1], None, IS_EQUAL
            )

        nc.sync.dma_start(b_rows[0:P:BLOCK, :], b.rearrange("(q i) o -> q (i o)", i=BLOCK))
        b_cols = held.tile([P, BLOCK], F32, name="b_cols", align_bytes=64)
        nc.vector.transpose(b_cols[:], b_rows[:])
        bias = b_cols[:, 0:1]

        idle_bank = psum.tile([P, WARM_COLUMNS], F32, name="idle_bank")
        zero_weights = zeros[:, 0:1].to_broadcast([P, P])
        zero_columns = zeros[:, 0:1].to_broadcast([P, WARM_COLUMNS])
        for i in range(WARM_MATMULS):
            nc.tensor.matmul(idle_bank[:], zero_weights, zero_columns, start=True, stop=True)

        window = psum.tile([P, S], F32, name="window")
        nc.tensor.matmul(window[:], ident[:], base_sb[:], start=True, stop=False)

        for e in range(E):
            piece = offsets[:, e * QC : (e + 1) * QC]
            for kb in range(KB):
                nc.tensor.matmul(
                    window[:].indirect(piece),
                    w_sb[e // PAIR][:, e % PAIR, kb, :],
                    x_sb[:, kb, e * Q : (e + 1) * Q],
                    start=False,
                    stop=(e == E - 1 and kb == KB - 1),
                )

        for h in range(S // HALF):
            columns = slice(h * HALF, (h + 1) * HALF)
            result = held.tile([P, HALF], F32, name="result%d" % h, align_bytes=KIB)
            nc.scalar.activation(result[:], window[:, columns], TANH, bias=bias)
            nc.scalar.dma_start(out[:, columns], result[:])
